import numpy as np
import ml_dtypes


def mxq(x, axis, fmt="e4m3"):
    dtype, down = {"e4m3": (ml_dtypes.float8_e4m3fn, 7), "e5m2": (ml_dtypes.float8_e5m2, 14)}[fmt]
    v = np.moveaxis(np.asarray(x, np.float32).astype(ml_dtypes.bfloat16).astype(np.float64), axis, -1)
    blocks = v.reshape(v.shape[:-1] + (-1, 32))
    amax = np.abs(blocks).max(-1, keepdims=True)
    byte = np.maximum(np.where(amax > 0, np.frexp(amax)[1] - 1 + 127, 0) - down, 1)
    scale = np.exp2(byte - 127.0)
    codes = (blocks / scale).astype(np.float32).astype(dtype).astype(np.float64)
    return np.moveaxis((codes * scale).reshape(v.shape), -1, axis)


WIDE = False


def mx_kscale(k):
    if not WIDE:
        return np.ones(k)
    levels = np.array([10, -10, 5, -5, 0])
    if k % 512:
        return np.exp2(np.random.permutation(np.resize(levels, k // 32))).repeat(32)
    a = np.empty((k // 512, 16))
    for p in range(k // 512):
        a[p, :8] = np.random.permutation(np.resize(levels, 8))
        for g in range(8):
            far = levels[np.abs(levels - a[p, g]) >= 10]
            a[p, g + 8] = far[np.random.randint(len(far))]
    return np.exp2(a.ravel()).repeat(32)


def f64(x):
    return np.asarray(x).astype(np.float64)


def striped(idx):
    return np.tile(idx.reshape(-1, 16).T, (8, 1)).astype(np.uint16)


def unstriped(offs):
    return offs[:16].T.reshape(-1).astype(np.int64)


E2M1 = np.array([0.0, 0.5, 1.0, 1.5, 2.0, 3.0, 4.0, 6.0, -0.0, -0.5, -1.0, -1.5, -2.0, -3.0, -4.0, -6.0])


def pack_weight(w, fmt):
    k, n = w.shape
    w = f64(np.asarray(w, np.float32).astype(ml_dtypes.bfloat16)).reshape(k // 32, 32, n)
    amax = np.abs(w).max(1)
    if fmt == "e4m3":
        byte = np.frexp(amax)[1] - 1 + 127 - 7
    else:
        mant, ex = np.frexp(amax / 6.0)
        byte = np.where(mant > 0.5, ex, ex - 1) + 127
    byte = np.clip(np.where(amax > 0, byte, 1), 1, 254)
    scaled = (w * np.exp2(127.0 - byte)[:, None, :]).reshape(k, n).astype(np.float32)
    by_word = np.ascontiguousarray(scaled.reshape(k // 512, 128, 4, n).transpose(0, 1, 3, 2))
    if fmt == "e4m3":
        words = by_word.astype(ml_dtypes.float8_e4m3fn).view(np.uint8)
    else:
        c = by_word.astype(ml_dtypes.float4_e2m1fn).view(np.uint8) & 0xF
        words = (c[..., 0::2] | (c[..., 1::2] << 4)).reshape(k // 512, 128, 2 * n)
    return np.ascontiguousarray(words), np.ascontiguousarray(byte.astype(np.uint8).reshape(k // 512, 16, n))


def unpack_weight(words, scales, fmt):
    g, _, n = scales.shape
    words = np.ascontiguousarray(words).reshape(g, 128, n, -1)
    if fmt == "e4m3":
        vals = words.view(ml_dtypes.float8_e4m3fn).astype(np.float64)
    else:
        nib = np.empty((g, 128, n, 4), np.uint8)
        nib[..., 0::2] = words & 0xF
        nib[..., 1::2] = words >> 4
        vals = E2M1[nib]
    vals = vals * np.repeat(np.exp2(scales.astype(np.float64) - 127.0), 8, axis=1)[..., None]
    return vals.transpose(0, 1, 3, 2).reshape(g * 512, n)


def gelu(v):
    return 0.5 * v * (1.0 + np.tanh(np.sqrt(2.0 / np.pi) * (v + 0.044715 * v**3)))


K, T, S, S2 = 1024, 4096, 1024, 512

def setup_inputs():
    n = np.random.standard_normal
    s = mx_kscale(K)[:, None]
    d = {}
    d["tab_words"], d["tab_scales"] = pack_weight(n((K, T)) * s, "e4m3")
    d["offs"] = striped(np.random.permutation(T)[:S])
    d["offs2"] = striped(np.random.permutation(T)[:S2])
    d["w1"] = (n((K, K)) / K / s / s.T).astype(np.float32)
    d["w3_words"], d["w3_scales"] = pack_weight(n((K, S2)) * s, "e2m1")
    d["base"] = n(S2).astype(np.float32)
    return d

def reference(tab_words, tab_scales, offs, offs2, w1, w3_words, w3_scales, base):
    TW = unpack_weight(tab_words, tab_scales, "e4m3")
    v = TW[:, unstriped(offs)]
    v2 = TW[:, unstriped(offs2)]
    w1q = mxq(f64(w1), 0, "e4m3")
    w3 = unpack_weight(w3_words, w3_scales, "e2m1")
    h = np.abs(w1q.T @ v)
    hq = mxq(h, 0, "e4m3")
    e = v2.T @ hq
    skip = w3.T @ hq
    return np.maximum(e, skip) - f64(base)[:, None]

@@ -1,0 +1,275 @@
+from contextlib import ExitStack
+
+import concourse.mybir as mybir
+
+K, T, S, S2 = 1024, 4096, 1024, 512
+FLOPS = 2 * K * K * S + 2 * 2 * K * S2 * S
+
+F32 = mybir.dt.float32
+BF16 = mybir.dt.bfloat16
+I32 = mybir.dt.int32
+U32 = mybir.dt.uint32
+U16 = mybir.dt.uint16
+U8 = mybir.dt.uint8
+FP8X4 = mybir.dt.float8_e4m3fn_x4
+FP4X4 = mybir.dt.float4_e2m1fn_x4
+ACT = mybir.ActivationFunctionType
+ALU = mybir.AluOpType
+
+P = 128
+PACK = 4
+K_PASS = P * PACK
+PASSES = K // K_PASS
+BANK = 512
+HALF = 512
+JC = 128
+W_HALF = 256
+
+
+def tile_list_galvanic_couple_screening_kernel(
+    tc, tab_words, tab_scales, offs, offs2, w1, w3_words, w3_scales, base, out
+):
+    nc = tc.nc
+    with ExitStack() as ctx:
+        keep = ctx.enter_context(tc.tile_pool(name="keep", bufs=1))
+        stage = ctx.enter_context(tc.tile_pool(name="stage", bufs=3))
+        reuse = ctx.enter_context(tc.tile_pool(name="reuse", bufs=1))
+        psum = ctx.enter_context(tc.psum_pool(name="psum", bufs=8))
+
+        placed = {
+            "words_j00": 0,
+            "tab_plane": 1984,
+            "words_j10": 2048,
+            "w_codes00": 4096,
+            "tab0": 8192,
+            "words_j01": 8192,
+            "words_j11": 10240,
+            "w_bf10": 12288,
+            "w_bf01": 16384,
+            "w_bf11": 20480,
+            "h_codes00": 20480,
+        }
+
+        def kept(shape, dtype, name, tag=""):
+            if name in placed:
+                return reuse.tile(shape, dtype, name=name, align_bytes=64, offset=placed[name])
+            return keep.tile(shape, dtype, name=name, tag=tag or name, align_bytes=64)
+
+        idx = keep.tile([P, S // 16], U16, name="idx")
+        idx2 = keep.tile([P, S2 // 16], U16, name="idx2")
+        nc.sync.dma_start(idx[:], offs)
+        nc.sync.dma_start(idx2[:], offs2)
+
+        tab_plane = kept([P, T], U8, "tab_plane")
+        w3_plane = kept([P, PASSES, S2], U8, "w3_plane")
+        nc.vector.memset(tab_plane[:].bitcast(I32), 0)
+        nc.gpsimd.memset(w3_plane[:].rearrange("p a c -> p (a c)").bitcast(I32), 0)
+
+        base_col = kept([P, S2 // P], F32, "base_col")
+        neg_base = kept([P, S2 // P], F32, "neg_base")
+        with nc.allow_non_contiguous_dma(reason="one value of base to a partition"):
+            nc.scalar.dma_start(base_col[:], base.rearrange("(c p) -> p c", p=P))
+        nc.scalar.activation(neg_base[:], base_col[:], ACT.Identity, scale=-1.0)
+
+        tab = [kept([P, T], I32, f"tab{a}") for a in range(PASSES)]
+        w_raw = {}
+
+        def load_table(a, c0, c1):
+            words = tab_words[a].rearrange("p n t -> p (n t)").bitcast(I32)
+            nc.sync.dma_start(tab[a][:, c0:c1], words[:, c0:c1])
+
+        def load_w1(a, b):
+            for u in range(2):
+                raw = kept([P, PACK, W_HALF], F32, f"w_raw{a}{b}{u}")
+                c0 = K_PASS * b + W_HALF * u
+                rows = w1[K_PASS * a : K_PASS * (a + 1), c0 : c0 + W_HALF]
+                nc.sync.dma_start(raw[:], rows.rearrange("(p j) c -> p j c", j=PACK))
+                w_raw[a, b, u] = raw
+
+        load_table(0, 0, T // 2)
+        for q in range(4):
+            nc.sync.dma_start(
+                tab_plane[32 * q : 32 * q + 8, :].bitcast(I32),
+                tab_scales[:, 4 * q : 4 * q + 4, :].bitcast(I32),
+            )
+        load_table(0, T // 2, T)
+        load_w1(0, 0)
+        load_table(1, 0, T)
+        load_w1(1, 0)
+        load_w1(0, 1)
+        load_w1(1, 1)
+        w3 = kept([P, PASSES, 2 * S2], U8, "w3")
+        nc.sync.dma_start(w3[:].bitcast(I32), w3_words.rearrange("a p c -> p a c").bitcast(I32))
+
+        for q in range(4):
+            nc.sync.dma_start(
+                w3_plane[32 * q : 32 * q + 4, :, :].bitcast(I32),
+                w3_scales[:, 4 * q : 4 * q + 4, :].rearrange("a r c -> r a c").bitcast(I32),
+            )
+
+        v_words = {}
+        v_plane = {}
+
+        def gather_words(name, a, offsets, tag=""):
+            words = kept([P, HALF], U32, f"words_{name}{a}", tag)
+            nc.vector.tensor_copy(words[:], tab[a][:].bitcast(U32).indirect(offsets))
+            v_words[name, a] = words
+
+        def gather_scales(name, offsets):
+            plane = kept([P, HALF], U8, f"plane_{name}")
+            nc.vector.tensor_copy(plane[:], tab_plane[:].indirect(offsets))
+            v_plane[name] = plane
+
+        lists = {"j0": idx[:, 0:32], "j1": idx[:, 32:64], "m": idx2[:]}
+
+        w_bf = {}
+        w_codes = {}
+        w_plane = {}
+
+        def cast_w1(a, b, u, engine):
+            if (a, b) not in w_bf:
+                w_bf[a, b] = kept([P, PACK, P, PACK], BF16, f"w_bf{a}{b}")
+            m0 = (W_HALF // PACK) * u
+            dst = w_bf[a, b][:, :, m0 : m0 + W_HALF // PACK, :].rearrange("p t m j -> p m t j")
+            src = w_raw[a, b, u][:].rearrange("p j (m t) -> p m t j", t=PACK)
+            if engine == "scalar":
+                nc.scalar.copy(dst, src)
+            else:
+                nc.vector.tensor_copy(dst, src)
+
+        def quantise_w1(a, b):
+            codes = kept([P, K_PASS], U32, f"w_codes{a}{b}")
+            plane = kept([P, K_PASS], U8, f"w_plane{a}{b}")
+            flat = w_bf[a, b][:].rearrange("p t m j -> p (t m j)")
+            for u in range(2):
+                cols = slice(256 * u, 256 * (u + 1))
+                nc.vector.quantize_mx(
+                    out=codes[:, cols].bitcast(FP8X4), scales=plane[:, cols], in_=flat[:, 1024 * u : 1024 * (u + 1)]
+                )
+            w_codes[a, b] = codes
+            w_plane[a, b] = plane
+
+        h_codes = {}
+        h_plane = {}
+        h_bank = {}
+
+        def state_pass(a, b, jc):
+            if a == 0:
+                h_bank[b, jc] = psum.tile([P, BANK], F32, name="bank")
+            name = f"j{jc // 4}"
+            cols = slice(JC * (jc % 4), JC * (jc % 4 + 1))
+            for t in range(PACK):
+                m_cols = slice(P * t, P * (t + 1))
+                nc.tensor.matmul_mx(
+                    out=h_bank[b, jc][:, JC * t : JC * (t + 1)],
+                    lhsT=w_codes[a, b][:, m_cols].bitcast(FP8X4),
+                    lhsT_scale=w_plane[a, b][:, m_cols],
+                    rhs=v_words[name, a][:, cols].bitcast(FP8X4),
+                    rhs_scale=v_plane[name][4 * a : P, cols],
+                    start=(a == 0 and t == 0),
+                    stop=(a == PASSES - 1 and t == PACK - 1),
+                )
+
+        h_bf = {}
+
+        def abs_state(b, jc):
+            jh = jc // 4
+            if (b, jh) not in h_bf:
+                h_bf[b, jh] = kept([P, HALF, PACK], BF16, f"h_bf{b}{jh}")
+            cols = slice(JC * (jc % 4), JC * (jc % 4 + 1))
+            nc.scalar.activation(
+                h_bf[b, jh][:, cols, :], h_bank[b, jc][:].rearrange("p (t n) -> p n t", t=PACK), ACT.Abs
+            )
+
+        def quantise_state(b, jh, c0, c1, tag=""):
+            if (b, jh) not in h_codes:
+                h_codes[b, jh] = kept([P, HALF], U32, f"h_codes{b}{jh}", tag)
+                h_plane[b, jh] = kept([P, HALF], U8, f"h_plane{b}{jh}")
+            nc.vector.quantize_mx(
+                out=h_codes[b, jh][:, c0:c1].bitcast(FP8X4),
+                scales=h_plane[b, jh][:, c0:c1],
+                in_=h_bf[b, jh][:, c0:c1, :].rearrange("p n t -> p (n t)"),
+            )
+
+        score = {}
+
+        def score_pass(kind, mt, jh, b):
+            if b == 0:
+                score[kind, mt, jh] = psum.tile([P, BANK], F32, name="bank")
+            m_cols = slice(P * mt, P * (mt + 1))
+            if kind == "e":
+                lhsT = v_words["m", b][:, m_cols].bitcast(FP8X4)
+                lhsT_scale = v_plane["m"][4 * b : P, m_cols]
+            else:
+                lhsT = w3[:, b, 2 * P * mt : 2 * P * (mt + 1)].bitcast(FP4X4)
+                lhsT_scale = w3_plane[:, b, m_cols]
+            nc.tensor.matmul_mx(
+                out=score[kind, mt, jh][:],
+                lhsT=lhsT,
+                lhsT_scale=lhsT_scale,
+                rhs=h_codes[b, jh][:].bitcast(FP8X4),
+                rhs_scale=h_plane[b, jh][:],
+                start=(b == 0),
+                stop=(b == PASSES - 1),
+            )
+
+        def finish_score(mt, jh, pieces):
+            width = HALF // pieces
+            for u in range(pieces):
+                cols = slice(width * u, width * (u + 1))
+                e_less = stage.tile([P, width], F32, name="e_less")
+                nc.scalar.activation(
+                    e_less[:], score["e", mt, jh][:, cols], ACT.Identity, bias=neg_base[:, mt : mt + 1]
+                )
+                res = stage.tile([P, width], F32, name="res", bufs=4)
+                nc.vector.scalar_tensor_tensor(
+                    out=res[:],
+                    in0=score["skip", mt, jh][:, cols],
+                    scalar=neg_base[:, mt : mt + 1],
+                    in1=e_less[:],
+                    op0=ALU.add,
+                    op1=ALU.max,
+                )
+                c0 = HALF * jh + width * u
+                nc.sync.dma_start(out[P * mt : P * (mt + 1), c0 : c0 + width], res[:])
+
+        gather_scales("j0", lists["j0"])
+        gather_scales("j1", lists["j1"])
+        gather_words("j0", 0, lists["j0"])
+        gather_words("j1", 0, lists["j1"])
+        cast_w1(0, 0, 0, "scalar")
+        cast_w1(0, 0, 1, "scalar")
+        quantise_w1(0, 0)
+        gather_scales("m", lists["m"])
+        gather_words("m", 0, lists["m"])
+        for jc in range(8):
+            state_pass(0, 0, jc)
+        gather_words("j0", 1, lists["j0"])
+        gather_words("j1", 1, lists["j1"])
+        cast_w1(1, 0, 0, "scalar")
+        cast_w1(1, 0, 1, "vector")
+        quantise_w1(1, 0)
+        cast_w1(0, 1, 0, "vector")
+        cast_w1(0, 1, 1, "vector")
+        quantise_w1(0, 1)
+        cast_w1(1, 1, 0, "vector")
+        cast_w1(1, 1, 1, "vector")
+        quantise_w1(1, 1)
+        for jc in range(8):
+            state_pass(1, 0, jc)
+            abs_state(0, jc)
+        quantise_state(0, 0, 0, HALF, "w_bf11")
+        gather_words("m", 1, lists["m"], "w_raw111")
+        for jc in range(8):
+            state_pass(0, 1, jc)
+            state_pass(1, 1, jc)
+            abs_state(1, jc)
+            quantise_state(1, jc // 4, JC * (jc % 4), JC * (jc % 4 + 1))
+            if jc == 3:
+                quantise_state(0, 1, 0, HALF, "w_raw110")
+        for jh in range(2):
+            for mt in range(4):
+                for kind in ("e", "skip"):
+                    score_pass(kind, mt, jh, 0)
+                    score_pass(kind, mt, jh, 1)
+                finish_score(mt, jh, 2 if (jh, mt) == (1, 3) else 1)

@@ -40,14 +40,15 @@ def tile_list_galvanic_couple_screening_kernel(
             "words_j00": 0,
             "tab_plane": 1984,
             "words_j10": 2048,
-            "w_codes00": 4096,
+            "words_m0": 4096,
+            "w_codes00": 6208,
             "tab0": 8192,
-            "words_j01": 8192,
-            "words_j11": 10240,
-            "w_bf10": 12288,
-            "w_bf01": 16384,
-            "w_bf11": 20480,
-            "h_codes00": 20480,
+            "words_j01": 8256,
+            "words_j11": 10304,
+            "w_bf10": 12352,
+            "w_bf01": 16448,
+            "w_bf11": 20544,
+            "h_codes00": 20544,
         }
 
         def kept(shape, dtype, name, tag=""):
@@ -63,13 +64,10 @@ def tile_list_galvanic_couple_screening_kernel(
         tab_plane = kept([P, T], U8, "tab_plane")
         w3_plane = kept([P, PASSES, S2], U8, "w3_plane")
         nc.vector.memset(tab_plane[:].bitcast(I32), 0)
-        nc.gpsimd.memset(w3_plane[:].rearrange("p a c -> p (a c)").bitcast(I32), 0)
+        nc.vector.memset(w3_plane[:].rearrange("p a c -> p (a c)").bitcast(I32), 0)
 
         base_col = kept([P, S2 // P], F32, "base_col")
         neg_base = kept([P, S2 // P], F32, "neg_base")
-        with nc.allow_non_contiguous_dma(reason="one value of base to a partition"):
-            nc.scalar.dma_start(base_col[:], base.rearrange("(c p) -> p c", p=P))
-        nc.scalar.activation(neg_base[:], base_col[:], ACT.Identity, scale=-1.0)
 
         tab = [kept([P, T], I32, f"tab{a}") for a in range(PASSES)]
         w_raw = {}
@@ -78,26 +76,27 @@ def tile_list_galvanic_couple_screening_kernel(
             words = tab_words[a].rearrange("p n t -> p (n t)").bitcast(I32)
             nc.sync.dma_start(tab[a][:, c0:c1], words[:, c0:c1])
 
-        def load_w1(a, b):
-            for u in range(2):
-                raw = kept([P, PACK, W_HALF], F32, f"w_raw{a}{b}{u}")
-                c0 = K_PASS * b + W_HALF * u
-                rows = w1[K_PASS * a : K_PASS * (a + 1), c0 : c0 + W_HALF]
+        def load_w1(a, b, pieces):
+            width = K_PASS // pieces
+            for v in range(pieces):
+                raw = kept([P, PACK, width], F32, f"w_raw{a}{b}{v}")
+                c0 = K_PASS * b + width * v
+                rows = w1[K_PASS * a : K_PASS * (a + 1), c0 : c0 + width]
                 nc.sync.dma_start(raw[:], rows.rearrange("(p j) c -> p j c", j=PACK))
-                w_raw[a, b, u] = raw
+                for c in range(0, width, W_HALF):
+                    w_raw[a, b, (width * v + c) // W_HALF] = raw[:, :, c : c + W_HALF]
 
-        load_table(0, 0, T // 2)
         for q in range(4):
-            nc.sync.dma_start(
+            nc.gpsimd.dma_start(
                 tab_plane[32 * q : 32 * q + 8, :].bitcast(I32),
                 tab_scales[:, 4 * q : 4 * q + 4, :].bitcast(I32),
             )
-        load_table(0, T // 2, T)
-        load_w1(0, 0)
+        load_table(0, 0, T)
+        load_w1(0, 0, 1)
         load_table(1, 0, T)
-        load_w1(1, 0)
-        load_w1(0, 1)
-        load_w1(1, 1)
+        load_w1(1, 0, 2)
+        load_w1(0, 1, 2)
+        load_w1(1, 1, 2)
         w3 = kept([P, PASSES, 2 * S2], U8, "w3")
         nc.sync.dma_start(w3[:].bitcast(I32), w3_words.rearrange("a p c -> p a c").bitcast(I32))
 
@@ -106,6 +105,10 @@ def tile_list_galvanic_couple_screening_kernel(
                 w3_plane[32 * q : 32 * q + 4, :, :].bitcast(I32),
                 w3_scales[:, 4 * q : 4 * q + 4, :].rearrange("a r c -> r a c").bitcast(I32),
             )
+
+        with nc.allow_non_contiguous_dma(reason="one value of base to a partition"):
+            nc.sync.dma_start(base_col[:], base.rearrange("(c p) -> p c", p=P))
+        nc.gpsimd.tensor_scalar(neg_base[:], base_col[:], -1.0, 0.0, ALU.mult, ALU.add)
 
         v_words = {}
         v_plane = {}
@@ -131,9 +134,9 @@ def tile_list_galvanic_couple_screening_kernel(
                 w_bf[a, b] = kept([P, PACK, P, PACK], BF16, f"w_bf{a}{b}")
             m0 = (W_HALF // PACK) * u
             dst = w_bf[a, b][:, :, m0 : m0 + W_HALF // PACK, :].rearrange("p t m j -> p m t j")
-            src = w_raw[a, b, u][:].rearrange("p j (m t) -> p m t j", t=PACK)
+            src = w_raw[a, b, u].rearrange("p j (m t) -> p m t j", t=PACK)
             if engine == "scalar":
-                nc.scalar.copy(dst, src)
+                nc.scalar.activation(dst, src, ACT.Copy)
             else:
                 nc.vector.tensor_copy(dst, src)
 
@@ -235,13 +238,13 @@ def tile_list_galvanic_couple_screening_kernel(
 
         gather_scales("j0", lists["j0"])
         gather_scales("j1", lists["j1"])
+        gather_scales("m", lists["m"])
         gather_words("j0", 0, lists["j0"])
         gather_words("j1", 0, lists["j1"])
+        gather_words("m", 0, lists["m"])
         cast_w1(0, 0, 0, "scalar")
         cast_w1(0, 0, 1, "scalar")
         quantise_w1(0, 0)
-        gather_scales("m", lists["m"])
-        gather_words("m", 0, lists["m"])
         for jc in range(8):
             state_pass(0, 0, jc)
         gather_words("j0", 1, lists["j0"])

@@ -24,6 +24,7 @@ BANK = 512
 HALF = 512
 JC = 128
 W_HALF = 256
+TAB_HEAD = 512
 
 
 def tile_list_galvanic_couple_screening_kernel(
@@ -37,18 +38,17 @@ def tile_list_galvanic_couple_screening_kernel(
         psum = ctx.enter_context(tc.psum_pool(name="psum", bufs=8))
 
         placed = {
-            "words_j00": 0,
-            "tab_plane": 1984,
-            "words_j10": 2048,
-            "words_m0": 4096,
-            "w_codes00": 6208,
-            "tab0": 8192,
-            "words_j01": 8256,
-            "words_j11": 10304,
-            "w_bf10": 12352,
-            "w_bf01": 16448,
-            "w_bf11": 20544,
-            "h_codes00": 20544,
+            "tab_plane": 0,
+            "words_j0": 0,
+            "tab0": 4096,
+            "words_j1": 4096,
+            "w_bf100": 8192,
+            "w_bf101": 10240,
+            "w_bf010": 12288,
+            "w_bf011": 14336,
+            "w_bf110": 16384,
+            "w_bf111": 18432,
+            "h_codes00": 18432,
         }
 
         def kept(shape, dtype, name, tag=""):
@@ -58,17 +58,12 @@ def tile_list_galvanic_couple_screening_kernel(
 
         idx = keep.tile([P, S // 16], U16, name="idx")
         idx2 = keep.tile([P, S2 // 16], U16, name="idx2")
-        nc.sync.dma_start(idx[:], offs)
-        nc.sync.dma_start(idx2[:], offs2)
-
         tab_plane = kept([P, T], U8, "tab_plane")
         w3_plane = kept([P, PASSES, S2], U8, "w3_plane")
         nc.vector.memset(tab_plane[:].bitcast(I32), 0)
         nc.vector.memset(w3_plane[:].rearrange("p a c -> p (a c)").bitcast(I32), 0)
-
         base_col = kept([P, S2 // P], F32, "base_col")
         neg_base = kept([P, S2 // P], F32, "neg_base")
-
         tab = [kept([P, T], I32, f"tab{a}") for a in range(PASSES)]
         w_raw = {}
 
@@ -86,12 +81,15 @@ def tile_list_galvanic_couple_screening_kernel(
                 for c in range(0, width, W_HALF):
                     w_raw[a, b, (width * v + c) // W_HALF] = raw[:, :, c : c + W_HALF]
 
+        nc.sync.dma_start(idx[:], offs)
+        nc.sync.dma_start(idx2[:], offs2)
+        load_table(0, 0, TAB_HEAD)
         for q in range(4):
-            nc.gpsimd.dma_start(
+            nc.sync.dma_start(
                 tab_plane[32 * q : 32 * q + 8, :].bitcast(I32),
                 tab_scales[:, 4 * q : 4 * q + 4, :].bitcast(I32),
             )
-        load_table(0, 0, T)
+        load_table(0, TAB_HEAD, T)
         load_w1(0, 0, 1)
         load_table(1, 0, T)
         load_w1(1, 0, 2)
@@ -99,42 +97,32 @@ def tile_list_galvanic_couple_screening_kernel(
         load_w1(1, 1, 2)
         w3 = kept([P, PASSES, 2 * S2], U8, "w3")
         nc.sync.dma_start(w3[:].bitcast(I32), w3_words.rearrange("a p c -> p a c").bitcast(I32))
-
         for q in range(4):
             nc.sync.dma_start(
                 w3_plane[32 * q : 32 * q + 4, :, :].bitcast(I32),
                 w3_scales[:, 4 * q : 4 * q + 4, :].rearrange("a r c -> r a c").bitcast(I32),
             )
-
         with nc.allow_non_contiguous_dma(reason="one value of base to a partition"):
             nc.sync.dma_start(base_col[:], base.rearrange("(c p) -> p c", p=P))
         nc.gpsimd.tensor_scalar(neg_base[:], base_col[:], -1.0, 0.0, ALU.mult, ALU.add)
 
-        v_words = {}
-        v_plane = {}
+        def gather_words(dst, a, offsets):
+            nc.vector.tensor_copy(dst, tab[a][:].bitcast(U32).indirect(offsets))
 
-        def gather_words(name, a, offsets, tag=""):
-            words = kept([P, HALF], U32, f"words_{name}{a}", tag)
-            nc.vector.tensor_copy(words[:], tab[a][:].bitcast(U32).indirect(offsets))
-            v_words[name, a] = words
-
-        def gather_scales(name, offsets):
-            plane = kept([P, HALF], U8, f"plane_{name}")
-            nc.vector.tensor_copy(plane[:], tab_plane[:].indirect(offsets))
-            v_plane[name] = plane
-
-        lists = {"j0": idx[:, 0:32], "j1": idx[:, 32:64], "m": idx2[:]}
+        def gather_scales(dst, offsets):
+            nc.vector.tensor_copy(dst, tab_plane[:].indirect(offsets))
 
         w_bf = {}
         w_codes = {}
         w_plane = {}
 
-        def cast_w1(a, b, u, engine):
-            if (a, b) not in w_bf:
-                w_bf[a, b] = kept([P, PACK, P, PACK], BF16, f"w_bf{a}{b}")
+        def cast_w1(a, b, u, pair, engine):
+            if (a, b, pair) not in w_bf:
+                w_bf[a, b, pair] = kept([P, 2, P, PACK], BF16, f"w_bf{a}{b}{pair}")
             m0 = (W_HALF // PACK) * u
-            dst = w_bf[a, b][:, :, m0 : m0 + W_HALF // PACK, :].rearrange("p t m j -> p m t j")
-            src = w_raw[a, b, u].rearrange("p j (m t) -> p m t j", t=PACK)
+            ts = slice(2 * pair, 2 * pair + 2)
+            dst = w_bf[a, b, pair][:, :, m0 : m0 + W_HALF // PACK, :].rearrange("p t m j -> p m j t")
+            src = w_raw[a, b, u].rearrange("p j (m t) -> p m j t", t=PACK)[:, :, :, ts]
             if engine == "scalar":
                 nc.scalar.activation(dst, src, ACT.Copy)
             else:
@@ -143,11 +131,12 @@ def tile_list_galvanic_couple_screening_kernel(
         def quantise_w1(a, b):
             codes = kept([P, K_PASS], U32, f"w_codes{a}{b}")
             plane = kept([P, K_PASS], U8, f"w_plane{a}{b}")
-            flat = w_bf[a, b][:].rearrange("p t m j -> p (t m j)")
-            for u in range(2):
-                cols = slice(256 * u, 256 * (u + 1))
+            for pair in range(2):
+                cols = slice(256 * pair, 256 * (pair + 1))
                 nc.vector.quantize_mx(
-                    out=codes[:, cols].bitcast(FP8X4), scales=plane[:, cols], in_=flat[:, 1024 * u : 1024 * (u + 1)]
+                    out=codes[:, cols].bitcast(FP8X4),
+                    scales=plane[:, cols],
+                    in_=w_bf[a, b, pair][:].rearrange("p t m j -> p (t m j)"),
                 )
             w_codes[a, b] = codes
             w_plane[a, b] = plane
@@ -155,25 +144,23 @@ def tile_list_galvanic_couple_screening_kernel(
         h_codes = {}
         h_plane = {}
         h_bank = {}
+        h_bf = {}
 
         def state_pass(a, b, jc):
             if a == 0:
                 h_bank[b, jc] = psum.tile([P, BANK], F32, name="bank")
-            name = f"j{jc // 4}"
-            cols = slice(JC * (jc % 4), JC * (jc % 4 + 1))
+            cols = slice(JC * jc, JC * (jc + 1))
             for t in range(PACK):
                 m_cols = slice(P * t, P * (t + 1))
                 nc.tensor.matmul_mx(
                     out=h_bank[b, jc][:, JC * t : JC * (t + 1)],
                     lhsT=w_codes[a, b][:, m_cols].bitcast(FP8X4),
                     lhsT_scale=w_plane[a, b][:, m_cols],
-                    rhs=v_words[name, a][:, cols].bitcast(FP8X4),
-                    rhs_scale=v_plane[name][4 * a : P, cols],
+                    rhs=words_j[a][:, cols].bitcast(FP8X4),
+                    rhs_scale=plane_j[4 * a : P, cols],
                     start=(a == 0 and t == 0),
                     stop=(a == PASSES - 1 and t == PACK - 1),
                 )
-
-        h_bf = {}
 
         def abs_state(b, jc):
             jh = jc // 4
@@ -201,8 +188,8 @@ def tile_list_galvanic_couple_screening_kernel(
                 score[kind, mt, jh] = psum.tile([P, BANK], F32, name="bank")
             m_cols = slice(P * mt, P * (mt + 1))
             if kind == "e":
-                lhsT = v_words["m", b][:, m_cols].bitcast(FP8X4)
-                lhsT_scale = v_plane["m"][4 * b : P, m_cols]
+                lhsT = words_m[b][:, m_cols].bitcast(FP8X4)
+                lhsT_scale = plane_m[4 * b : P, m_cols]
             else:
                 lhsT = w3[:, b, 2 * P * mt : 2 * P * (mt + 1)].bitcast(FP4X4)
                 lhsT_scale = w3_plane[:, b, m_cols]
@@ -236,40 +223,50 @@ def tile_list_galvanic_couple_screening_kernel(
                 c0 = HALF * jh + width * u
                 nc.sync.dma_start(out[P * mt : P * (mt + 1), c0 : c0 + width], res[:])
 
-        gather_scales("j0", lists["j0"])
-        gather_scales("j1", lists["j1"])
-        gather_scales("m", lists["m"])
-        gather_words("j0", 0, lists["j0"])
-        gather_words("j1", 0, lists["j1"])
-        gather_words("m", 0, lists["m"])
-        cast_w1(0, 0, 0, "scalar")
-        cast_w1(0, 0, 1, "scalar")
+        plane_j = kept([P, S], U8, "plane_j")
+        plane_m = kept([P, S2], U8, "plane_m")
+        gather_scales(plane_j[:], idx[:])
+        gather_scales(plane_m[:], idx2[:])
+        words_j = [kept([P, S], U32, f"words_j{a}") for a in range(PASSES)]
+        gather_words(words_j[0][:], 0, idx[:])
+        for u in range(2):
+            for pair in range(2):
+                cast_w1(0, 0, u, pair, "scalar")
         quantise_w1(0, 0)
+        words_m = [kept([P, S2], U32, "words_m0")]
+        gather_words(words_m[0][:], 0, idx2[:])
         for jc in range(8):
             state_pass(0, 0, jc)
-        gather_words("j0", 1, lists["j0"])
-        gather_words("j1", 1, lists["j1"])
-        cast_w1(1, 0, 0, "scalar")
-        cast_w1(1, 0, 1, "vector")
+        for jh in range(2):
+            gather_words(words_j[1][:, HALF * jh : HALF * (jh + 1)], 1, idx[:, 32 * jh : 32 * (jh + 1)])
+        cast_w1(1, 0, 0, 0, "scalar")
+        cast_w1(1, 0, 0, 1, "scalar")
+        cast_w1(1, 0, 1, 0, "vector")
+        cast_w1(1, 0, 1, 1, "scalar")
         quantise_w1(1, 0)
-        cast_w1(0, 1, 0, "vector")
-        cast_w1(0, 1, 1, "vector")
+        cast_w1(0, 1, 0, 0, "vector")
+        cast_w1(0, 1, 0, 1, "scalar")
+        cast_w1(0, 1, 1, 0, "vector")
+        cast_w1(0, 1, 1, 1, "vector")
         quantise_w1(0, 1)
-        cast_w1(1, 1, 0, "vector")
-        cast_w1(1, 1, 1, "vector")
+        for u in range(2):
+            for pair in range(2):
+                cast_w1(1, 1, u, pair, "vector")
         quantise_w1(1, 1)
         for jc in range(8):
             state_pass(1, 0, jc)
             abs_state(0, jc)
-        quantise_state(0, 0, 0, HALF, "w_bf11")
-        gather_words("m", 1, lists["m"], "w_raw111")
+        quantise_state(0, 0, 0, HALF)
+        words_m.append(kept([P, S2], U32, "words_m1", "w_raw111"))
+        gather_words(words_m[1][:], 1, idx2[:])
         for jc in range(8):
             state_pass(0, 1, jc)
             state_pass(1, 1, jc)
             abs_state(1, jc)
-            quantise_state(1, jc // 4, JC * (jc % 4), JC * (jc % 4 + 1))
-            if jc == 3:
-                quantise_state(0, 1, 0, HALF, "w_raw110")
+            if jc < 4:
+                quantise_state(1, 0, JC * jc, JC * (jc + 1))
+        quantise_state(0, 1, 0, HALF, "h_bf10")
+        quantise_state(1, 1, 0, HALF)
         for jh in range(2):
             for mt in range(4):
                 for kind in ("e", "skip"):

from contextlib import ExitStack

import concourse.mybir as mybir

K, T, S, S2 = 1024, 4096, 1024, 512
FLOPS = 2 * K * K * S + 2 * 2 * K * S2 * S

F32 = mybir.dt.float32
BF16 = mybir.dt.bfloat16
I32 = mybir.dt.int32
U32 = mybir.dt.uint32
U16 = mybir.dt.uint16
U8 = mybir.dt.uint8
FP8X4 = mybir.dt.float8_e4m3fn_x4
FP4X4 = mybir.dt.float4_e2m1fn_x4
ACT = mybir.ActivationFunctionType
ALU = mybir.AluOpType

P = 128
PACK = 4
K_PASS = P * PACK
PASSES = K // K_PASS
BANK = 512
HALF = 512
JC = 128
W_HALF = 256
TAB_HEAD = 512


def tile_list_galvanic_couple_screening_kernel(
    tc, tab_words, tab_scales, offs, offs2, w1, w3_words, w3_scales, base, out
):
    nc = tc.nc
    with ExitStack() as ctx:
        keep = ctx.enter_context(tc.tile_pool(name="keep", bufs=1))
        stage = ctx.enter_context(tc.tile_pool(name="stage", bufs=3))
        reuse = ctx.enter_context(tc.tile_pool(name="reuse", bufs=1))
        psum = ctx.enter_context(tc.psum_pool(name="psum", bufs=8))

        placed = {
            "tab_plane": 0,
            "words_j0": 0,
            "tab0": 4096,
            "words_j1": 4096,
            "w_bf100": 8192,
            "w_bf101": 10240,
            "w_bf010": 12288,
            "w_bf011": 14336,
            "w_bf110": 16384,
            "w_bf111": 18432,
            "h_codes00": 18432,
        }

        def kept(shape, dtype, name, tag=""):
            if name in placed:
                return reuse.tile(shape, dtype, name=name, align_bytes=64, offset=placed[name])
            return keep.tile(shape, dtype, name=name, tag=tag or name, align_bytes=64)

        idx = keep.tile([P, S // 16], U16, name="idx")
        idx2 = keep.tile([P, S2 // 16], U16, name="idx2")
        tab_plane = kept([P, T], U8, "tab_plane")
        w3_plane = kept([P, PASSES, S2], U8, "w3_plane")
        nc.vector.memset(tab_plane[:].bitcast(I32), 0)
        nc.vector.memset(w3_plane[:].rearrange("p a c -> p (a c)").bitcast(I32), 0)
        base_col = kept([P, S2 // P], F32, "base_col")
        neg_base = kept([P, S2 // P], F32, "neg_base")
        tab = [kept([P, T], I32, f"tab{a}") for a in range(PASSES)]
        w_raw = {}

        def load_table(a, c0, c1):
            words = tab_words[a].rearrange("p n t -> p (n t)").bitcast(I32)
            nc.sync.dma_start(tab[a][:, c0:c1], words[:, c0:c1])

        def load_w1(a, b, pieces):
            width = K_PASS // pieces
            for v in range(pieces):
                raw = kept([P, PACK, width], F32, f"w_raw{a}{b}{v}")
                c0 = K_PASS * b + width * v
                rows = w1[K_PASS * a : K_PASS * (a + 1), c0 : c0 + width]
                nc.sync.dma_start(raw[:], rows.rearrange("(p j) c -> p j c", j=PACK))
                for c in range(0, width, W_HALF):
                    w_raw[a, b, (width * v + c) // W_HALF] = raw[:, :, c : c + W_HALF]

        nc.sync.dma_start(idx[:], offs)
        nc.sync.dma_start(idx2[:], offs2)
        load_table(0, 0, TAB_HEAD)
        for q in range(4):
            nc.sync.dma_start(
                tab_plane[32 * q : 32 * q + 8, :].bitcast(I32),
                tab_scales[:, 4 * q : 4 * q + 4, :].bitcast(I32),
            )
        load_table(0, TAB_HEAD, T)
        load_w1(0, 0, 1)
        load_table(1, 0, T)
        load_w1(1, 0, 2)
        load_w1(0, 1, 2)
        load_w1(1, 1, 2)
        w3 = kept([P, PASSES, 2 * S2], U8, "w3")
        nc.sync.dma_start(w3[:].bitcast(I32), w3_words.rearrange("a p c -> p a c").bitcast(I32))
        for q in range(4):
            nc.sync.dma_start(
                w3_plane[32 * q : 32 * q + 4, :, :].bitcast(I32),
                w3_scales[:, 4 * q : 4 * q + 4, :].rearrange("a r c -> r a c").bitcast(I32),
            )
        with nc.allow_non_contiguous_dma(reason="one value of base to a partition"):
            nc.sync.dma_start(base_col[:], base.rearrange("(c p) -> p c", p=P))
        nc.gpsimd.tensor_scalar(neg_base[:], base_col[:], -1.0, 0.0, ALU.mult, ALU.add)

        def gather_words(dst, a, offsets):
            nc.vector.tensor_copy(dst, tab[a][:].bitcast(U32).indirect(offsets))

        def gather_scales(dst, offsets):
            nc.vector.tensor_copy(dst, tab_plane[:].indirect(offsets))

        w_bf = {}
        w_codes = {}
        w_plane = {}

        def cast_w1(a, b, u, pair, engine):
            if (a, b, pair) not in w_bf:
                w_bf[a, b, pair] = kept([P, 2, P, PACK], BF16, f"w_bf{a}{b}{pair}")
            m0 = (W_HALF // PACK) * u
            ts = slice(2 * pair, 2 * pair + 2)
            dst = w_bf[a, b, pair][:, :, m0 : m0 + W_HALF // PACK, :].rearrange("p t m j -> p m j t")
            src = w_raw[a, b, u].rearrange("p j (m t) -> p m j t", t=PACK)[:, :, :, ts]
            if engine == "scalar":
                nc.scalar.activation(dst, src, ACT.Copy)
            else:
                nc.vector.tensor_copy(dst, src)

        def quantise_w1(a, b):
            codes = kept([P, K_PASS], U32, f"w_codes{a}{b}")
            plane = kept([P, K_PASS], U8, f"w_plane{a}{b}")
            for pair in range(2):
                cols = slice(256 * pair, 256 * (pair + 1))
                nc.vector.quantize_mx(
                    out=codes[:, cols].bitcast(FP8X4),
                    scales=plane[:, cols],
                    in_=w_bf[a, b, pair][:].rearrange("p t m j -> p (t m j)"),
                )
            w_codes[a, b] = codes
            w_plane[a, b] = plane

        h_codes = {}
        h_plane = {}
        h_bank = {}
        h_bf = {}

        def state_pass(a, b, jc):
            if a == 0:
                h_bank[b, jc] = psum.tile([P, BANK], F32, name="bank")
            cols = slice(JC * jc, JC * (jc + 1))
            for t in range(PACK):
                m_cols = slice(P * t, P * (t + 1))
                nc.tensor.matmul_mx(
                    out=h_bank[b, jc][:, JC * t : JC * (t + 1)],
                    lhsT=w_codes[a, b][:, m_cols].bitcast(FP8X4),
                    lhsT_scale=w_plane[a, b][:, m_cols],
                    rhs=words_j[a][:, cols].bitcast(FP8X4),
                    rhs_scale=plane_j[4 * a : P, cols],
                    start=(a == 0 and t == 0),
                    stop=(a == PASSES - 1 and t == PACK - 1),
                )

        def abs_state(b, jc):
            jh = jc // 4
            if (b, jh) not in h_bf:
                h_bf[b, jh] = kept([P, HALF, PACK], BF16, f"h_bf{b}{jh}")
            cols = slice(JC * (jc % 4), JC * (jc % 4 + 1))
            nc.scalar.activation(
                h_bf[b, jh][:, cols, :], h_bank[b, jc][:].rearrange("p (t n) -> p n t", t=PACK), ACT.Abs
            )

        def quantise_state(b, jh, c0, c1, tag=""):
            if (b, jh) not in h_codes:
                h_codes[b, jh] = kept([P, HALF], U32, f"h_codes{b}{jh}", tag)
                h_plane[b, jh] = kept([P, HALF], U8, f"h_plane{b}{jh}")
            nc.vector.quantize_mx(
                out=h_codes[b, jh][:, c0:c1].bitcast(FP8X4),
                scales=h_plane[b, jh][:, c0:c1],
                in_=h_bf[b, jh][:, c0:c1, :].rearrange("p n t -> p (n t)"),
            )

        score = {}

        def score_pass(kind, mt, jh, b):
            if b == 0:
                score[kind, mt, jh] = psum.tile([P, BANK], F32, name="bank")
            m_cols = slice(P * mt, P * (mt + 1))
            if kind == "e":
                lhsT = words_m[b][:, m_cols].bitcast(FP8X4)
                lhsT_scale = plane_m[4 * b : P, m_cols]
            else:
                lhsT = w3[:, b, 2 * P * mt : 2 * P * (mt + 1)].bitcast(FP4X4)
                lhsT_scale = w3_plane[:, b, m_cols]
            nc.tensor.matmul_mx(
                out=score[kind, mt, jh][:],
                lhsT=lhsT,
                lhsT_scale=lhsT_scale,
                rhs=h_codes[b, jh][:].bitcast(FP8X4),
                rhs_scale=h_plane[b, jh][:],
                start=(b == 0),
                stop=(b == PASSES - 1),
            )

        def finish_score(mt, jh, pieces):
            width = HALF // pieces
            for u in range(pieces):
                cols = slice(width * u, width * (u + 1))
                e_less = stage.tile([P, width], F32, name="e_less")
                nc.scalar.activation(
                    e_less[:], score["e", mt, jh][:, cols], ACT.Identity, bias=neg_base[:, mt : mt + 1]
                )
                res = stage.tile([P, width], F32, name="res", bufs=4)
                nc.vector.scalar_tensor_tensor(
                    out=res[:],
                    in0=score["skip", mt, jh][:, cols],
                    scalar=neg_base[:, mt : mt + 1],
                    in1=e_less[:],
                    op0=ALU.add,
                    op1=ALU.max,
                )
                c0 = HALF * jh + width * u
                nc.sync.dma_start(out[P * mt : P * (mt + 1), c0 : c0 + width], res[:])

        plane_j = kept([P, S], U8, "plane_j")
        plane_m = kept([P, S2], U8, "plane_m")
        gather_scales(plane_j[:], idx[:])
        gather_scales(plane_m[:], idx2[:])
        words_j = [kept([P, S], U32, f"words_j{a}") for a in range(PASSES)]
        gather_words(words_j[0][:], 0, idx[:])
        for u in range(2):
            for pair in range(2):
                cast_w1(0, 0, u, pair, "scalar")
        quantise_w1(0, 0)
        words_m = [kept([P, S2], U32, "words_m0")]
        gather_words(words_m[0][:], 0, idx2[:])
        for jc in range(8):
            state_pass(0, 0, jc)
        for jh in range(2):
            gather_words(words_j[1][:, HALF * jh : HALF * (jh + 1)], 1, idx[:, 32 * jh : 32 * (jh + 1)])
        cast_w1(1, 0, 0, 0, "scalar")
        cast_w1(1, 0, 0, 1, "scalar")
        cast_w1(1, 0, 1, 0, "vector")
        cast_w1(1, 0, 1, 1, "scalar")
        quantise_w1(1, 0)
        cast_w1(0, 1, 0, 0, "vector")
        cast_w1(0, 1, 0, 1, "scalar")
        cast_w1(0, 1, 1, 0, "vector")
        cast_w1(0, 1, 1, 1, "vector")
        quantise_w1(0, 1)
        for u in range(2):
            for pair in range(2):
                cast_w1(1, 1, u, pair, "vector")
        quantise_w1(1, 1)
        for jc in range(8):
            state_pass(1, 0, jc)
            abs_state(0, jc)
        quantise_state(0, 0, 0, HALF)
        words_m.append(kept([P, S2], U32, "words_m1", "w_raw111"))
        gather_words(words_m[1][:], 1, idx2[:])
        for jc in range(8):
            state_pass(0, 1, jc)
            state_pass(1, 1, jc)
            abs_state(1, jc)
            if jc < 4:
                quantise_state(1, 0, JC * jc, JC * (jc + 1))
        quantise_state(0, 1, 0, HALF, "h_bf10")
        quantise_state(1, 1, 0, HALF)
        for jh in range(2):
            for mt in range(4):
                for kind in ("e", "skip"):
                    score_pass(kind, mt, jh, 0)
                    score_pass(kind, mt, jh, 1)
                finish_score(mt, jh, 2 if (jh, mt) == (1, 3) else 1)
